import numpy as np
import ml_dtypes


def mxq(x, axis, fmt="e4m3"):
    dtype, down = {"e4m3": (ml_dtypes.float8_e4m3fn, 7), "e5m2": (ml_dtypes.float8_e5m2, 14)}[fmt]
    v = np.moveaxis(np.asarray(x, np.float32).astype(ml_dtypes.bfloat16).astype(np.float64), axis, -1)
    blocks = v.reshape(v.shape[:-1] + (-1, 32))
    amax = np.abs(blocks).max(-1, keepdims=True)
    byte = np.maximum(np.where(amax > 0, np.frexp(amax)[1] - 1 + 127, 0) - down, 1)
    scale = np.exp2(byte - 127.0)
    codes = (blocks / scale).astype(np.float32).astype(dtype).astype(np.float64)
    return np.moveaxis((codes * scale).reshape(v.shape), -1, axis)


WIDE = False


def mx_kscale(k):
    if not WIDE:
        return np.ones(k)
    levels = np.array([10, -10, 5, -5, 0])
    if k % 512:
        return np.exp2(np.random.permutation(np.resize(levels, k // 32))).repeat(32)
    a = np.empty((k // 512, 16))
    for p in range(k // 512):
        a[p, :8] = np.random.permutation(np.resize(levels, 8))
        for g in range(8):
            far = levels[np.abs(levels - a[p, g]) >= 10]
            a[p, g + 8] = far[np.random.randint(len(far))]
    return np.exp2(a.ravel()).repeat(32)


def f64(x):
    return np.asarray(x).astype(np.float64)


def striped(idx):
    return np.tile(idx.reshape(-1, 16).T, (8, 1)).astype(np.uint16)


def unstriped(offs):
    return offs[:16].T.reshape(-1).astype(np.int64)


E2M1 = np.array([0.0, 0.5, 1.0, 1.5, 2.0, 3.0, 4.0, 6.0, -0.0, -0.5, -1.0, -1.5, -2.0, -3.0, -4.0, -6.0])


def pack_weight(w, fmt):
    k, n = w.shape
    w = f64(np.asarray(w, np.float32).astype(ml_dtypes.bfloat16)).reshape(k // 32, 32, n)
    amax = np.abs(w).max(1)
    if fmt == "e4m3":
        byte = np.frexp(amax)[1] - 1 + 127 - 7
    else:
        mant, ex = np.frexp(amax / 6.0)
        byte = np.where(mant > 0.5, ex, ex - 1) + 127
    byte = np.clip(np.where(amax > 0, byte, 1), 1, 254)
    scaled = (w * np.exp2(127.0 - byte)[:, None, :]).reshape(k, n).astype(np.float32)
    by_word = np.ascontiguousarray(scaled.reshape(k // 512, 128, 4, n).transpose(0, 1, 3, 2))
    if fmt == "e4m3":
        words = by_word.astype(ml_dtypes.float8_e4m3fn).view(np.uint8)
    else:
        c = by_word.astype(ml_dtypes.float4_e2m1fn).view(np.uint8) & 0xF
        words = (c[..., 0::2] | (c[..., 1::2] << 4)).reshape(k // 512, 128, 2 * n)
    return np.ascontiguousarray(words), np.ascontiguousarray(byte.astype(np.uint8).reshape(k // 512, 16, n))


def unpack_weight(words, scales, fmt):
    g, _, n = scales.shape
    words = np.ascontiguousarray(words).reshape(g, 128, n, -1)
    if fmt == "e4m3":
        vals = words.view(ml_dtypes.float8_e4m3fn).astype(np.float64)
    else:
        nib = np.empty((g, 128, n, 4), np.uint8)
        nib[..., 0::2] = words & 0xF
        nib[..., 1::2] = words >> 4
        vals = E2M1[nib]
    vals = vals * np.repeat(np.exp2(scales.astype(np.float64) - 127.0), 8, axis=1)[..., None]
    return vals.transpose(0, 1, 3, 2).reshape(g * 512, n)


def gelu(v):
    return 0.5 * v * (1.0 + np.tanh(np.sqrt(2.0 / np.pi) * (v + 0.044715 * v**3)))


K, T, S, H, P = 512, 4096, 1024, 1024, 512


def setup_inputs():
    n = np.random.standard_normal
    s = mx_kscale(K)[:, None]
    u = mx_kscale(H)[:, None]
    tab_words, tab_scales = pack_weight(n((K, T)) * s, "e4m3")
    w3_words, w3_scales = pack_weight(n((K, H)) / np.sqrt(K) / s, "e4m3")
    wd_words, wd_scales = pack_weight(2.0 * n((H, H)) / np.sqrt(H) / u, "e2m1")
    return {
        "tab_words": tab_words, "tab_scales": tab_scales,
        "offs": striped(np.random.permutation(T)[:S]),
        "pos1": striped(np.random.permutation(S)[:P]),
        "w1": (n((K, H)) / np.sqrt(K) / s).astype(np.float32),
        "w2": (n((K, H)) / np.sqrt(K) / s).astype(np.float32),
        "w3_words": w3_words, "w3_scales": w3_scales,
        "gain": (np.exp(0.3 * n(H)) * u[:, 0]).astype(np.float32),
        "fade": np.exp(0.5 * n((H, P))).astype(np.float32),
        "wd_words": wd_words, "wd_scales": wd_scales,
        "base": (0.8 * n(H)).astype(np.float32),
        "skip": (0.9 * np.exp(0.3 * n(H)) / u[:, 0]).astype(np.float32),
        "wgo": np.exp(0.3 * n((128, P))).astype(np.float32),
    }


def reference(tab_words, tab_scales, offs, pos1, w1, w2, w3_words, w3_scales,
              gain, fade, wd_words, wd_scales, base, skip, wgo):
    v = unpack_weight(tab_words, tab_scales, "e4m3")[:, unstriped(offs)]
    d1 = mxq(f64(w1), 0, "e4m3").T @ v
    d2 = mxq(f64(w2), 0, "e4m3").T @ v
    d3 = unpack_weight(w3_words, w3_scales, "e4m3").T @ v
    h = f64(gain)[:, None] * np.tanh(np.minimum(d1, d2) + d3)
    x = h[:, unstriped(pos1)] * f64(fade)
    xq = mxq(x, 0, "e4m3")
    e = unpack_weight(wd_words, wd_scales, "e2m1").T @ xq
    y = 1.0 / (1.0 + np.exp(-(e + f64(base)[:, None])))
    out = f64(skip)[:, None] * h
    out[:, unstriped(pos1)] = np.tile(f64(wgo), (H // 128, 1)) * y
    return out

@@ -1,0 +1,345 @@
+from contextlib import ExitStack
+
+import concourse.mybir as mybir
+
+K, T, S, H, P = 512, 4096, 1024, 1024, 512
+FLOPS = 2 * (3 * K * H * S + H * H * P)
+
+F32 = mybir.dt.float32
+BF16 = mybir.dt.bfloat16
+I32 = mybir.dt.int32
+U32 = mybir.dt.uint32
+U16 = mybir.dt.uint16
+U8 = mybir.dt.uint8
+FP8X4 = mybir.dt.float8_e4m3fn_x4
+FP4X4 = mybir.dt.float4_e2m1fn_x4
+ALU = mybir.AluOpType
+ACT = mybir.ActivationFunctionType
+
+PARTS = 128
+PACK = 4
+PASS = PARTS * PACK
+PASSES = H // PASS
+TILES = H // PARTS
+BANK = 512
+HALVES = S // BANK
+CHUNK = P // 2
+SPLIT_TILES = 2
+
+
+def tile_list_autochrome_grain_features_kernel(
+    tc, tab_words, tab_scales, offs, pos1, w1, w2, w3_words, w3_scales,
+    gain, fade, wd_words, wd_scales, base, skip, wgo, out,
+):
+    nc = tc.nc
+    with ExitStack() as ctx:
+        keep = ctx.enter_context(tc.tile_pool(name="keep", bufs=1))
+        ring = ctx.enter_context(tc.tile_pool(name="ring", bufs=3))
+        pages = ctx.enter_context(tc.tile_pool(name="pages", bufs=4))
+        psum = ctx.enter_context(tc.psum_pool(name="psum", bufs=1))
+
+        def held(shape, dtype, name):
+            return keep.tile(shape, dtype, name=name, align_bytes=64)
+
+        offs_sb = keep.tile([PARTS, S // 16], U16, name="offs_sb")
+        pos_sb = keep.tile([PARTS, P // 16], U16, name="pos_sb")
+        tab_sb = held([PARTS, T], U32, "tab_sb")
+        tabs_sb = held([PARTS, T], U8, "tabs_sb")
+        w3s_raw = held([PARTS, H], U8, "w3s_raw")
+        w3s = held([PARTS, H], U8, "w3s")
+        wds_raw = held([PARTS, PASSES * H], U8, "wds_raw")
+        v_words = [held([PARTS, BANK], U32, f"v_words{h}") for h in range(HALVES)]
+        v_scales = held([PARTS, S], U8, "v_scales")
+
+        nc.vector.memset(tabs_sb[:].bitcast(I32), 0)
+        nc.gpsimd.memset(w3s_raw[:].bitcast(I32), 0)
+
+        def load_w(w, c0, width, name):
+            raw = held([PARTS, PACK, width], F32, name)
+            nc.sync.dma_start(out=raw[:], in_=w[:, c0 : c0 + width].rearrange("(p j) c -> p j c", j=PACK))
+            return raw
+
+        def load_w3(b):
+            raw = held([PARTS, PASS], I32, f"w3_raw{b}")
+            nc.sync.dma_start(
+                out=raw[:],
+                in_=w3_words[0].rearrange("p c i -> p (c i)")[:, 4 * PASS * b : 4 * PASS * (b + 1)].bitcast(I32),
+            )
+            return raw
+
+        def load_vec(vec, name):
+            sb = held([PARTS, PASSES, PACK], F32, name)
+            nc.sync.dma_start(out=sb[:], in_=vec.rearrange("(b p t) -> p b t", b=PASSES, t=PACK))
+            return sb
+
+        def load_fade(pair):
+            b, t = divmod(2 * pair, PACK)
+            sb = held([PARTS, 2, P], F32, f"fade{pair}")
+            nc.sync.dma_start(
+                out=sb[:],
+                in_=fade[PASS * b : PASS * (b + 1), :].rearrange("(p t) m -> p t m", t=PACK)[:, t : t + 2, :],
+            )
+            return sb
+
+        tabs_in = held([PARTS, T // 4], I32, "tabs_in")
+        for q in range(4):
+            nc.sync.dma_start(
+                out=tabs_in[32 * q : 32 * q + 4, :], in_=tab_scales[0, 4 * q : 4 * q + 4, :].bitcast(I32)
+            )
+        nc.gpsimd.memset(wds_raw[:].bitcast(I32), 0)
+
+        HW = PASS // 2
+        w1_raw = {}
+        w2_raw = {}
+        nc.sync.dma_start(offs_sb[:], offs)
+        nc.sync.dma_start(
+            out=tab_sb[:].bitcast(I32), in_=tab_words[0].rearrange("p t i -> p (t i)").bitcast(I32)
+        )
+        w1_raw[0, 0] = load_w(w1, 0, HW, "w1_raw00")
+        w1_raw[0, 1] = load_w(w1, HW, HW, "w1_raw01")
+        for q in range(4):
+            nc.sync.dma_start(
+                out=w3s_raw[32 * q : 32 * q + 4, :].bitcast(I32),
+                in_=w3_scales[0, 4 * q : 4 * q + 4, :].bitcast(I32),
+            )
+        w3_raw = {0: load_w3(0)}
+        w2_raw[0, 0] = load_w(w2, 0, HW, "w2_raw00")
+        w2_raw[0, 1] = load_w(w2, HW, HW, "w2_raw01")
+        gain_sb = load_vec(gain, "gain_sb")
+        nc.sync.dma_start(pos_sb[:], pos1)
+        fade_sb = [load_fade(0)]
+        for hh in range(2):
+            w1_raw[1, hh] = load_w(w1, PASS + hh * HW, HW, f"w1_raw1{hh}")
+        fade_sb.append(load_fade(1))
+        for hh in range(2):
+            w2_raw[1, hh] = load_w(w2, PASS + hh * HW, HW, f"w2_raw1{hh}")
+        w3_raw[1] = load_w3(1)
+        fade_sb.append(load_fade(2))
+        fade_sb.append(load_fade(3))
+        skip_sb = load_vec(skip, "skip_sb")
+        base_sb = load_vec(base, "base_sb")
+        wd_raw = held([PARTS, PASSES * H * 2], U8, "wd_raw")
+        nc.sync.dma_start(
+            out=wd_raw[:].bitcast(I32).rearrange("p (a n) -> p a n", a=PASSES),
+            in_=wd_words.bitcast(I32).rearrange("a p n -> p a n"),
+        )
+        for q in range(4):
+            nc.sync.dma_start(
+                out=wds_raw[32 * q : 32 * q + 4, :].bitcast(I32).rearrange("r (a n) -> r a n", a=PASSES),
+                in_=wd_scales[:, 4 * q : 4 * q + 4, :].bitcast(I32).rearrange("a r n -> r a n"),
+            )
+        wgo_sb = held([PARTS, PACK, P], F32, "wgo_sb")
+        for q in range(4):
+            nc.sync.dma_start(
+                out=wgo_sb[32 * q : 32 * q + 32], in_=wgo.rearrange("(p t) m -> p t m", t=PACK)
+            )
+
+        def cast_w(engine_copy, grouped, raw, hh):
+            mm = PARTS // 2
+            engine_copy(
+                grouped[:].rearrange("p (t m j) -> p m j t", t=PACK, j=PACK)[:, mm * hh : mm * (hh + 1)],
+                raw[:].rearrange("p j (m t) -> p m j t", t=PACK),
+            )
+
+        def mx_tiles(name, width):
+            return held([PARTS, width], U32, name + "_codes"), held([PARTS, width], U8, name + "_scales")
+
+        def quantize(tiles, src, c0, c1):
+            nc.vector.quantize_mx(out=tiles[0][:, c0:c1].bitcast(FP8X4), scales=tiles[1][:, c0:c1], in_=src)
+
+        def deal_w3(b):
+            dealt = held([PARTS, PASS], I32, f"w3_dealt{b}")
+            nc.vector.tensor_copy(
+                dealt[:].rearrange("p (t m) -> p m t", t=PACK), w3_raw[b][:].rearrange("p (m t) -> p m t", t=PACK)
+            )
+            return dealt
+
+        grouped = {(n, b): held([PARTS, PACK * PASS], BF16, f"grp{n}{b}") for n in (1, 2) for b in range(PASSES)}
+        wq = {(n, b): mx_tiles(f"wq{n}{b}", PASS) for n in (1, 2) for b in range(PASSES)}
+
+        for q in range(4):
+            nc.vector.tensor_copy(tabs_sb[32 * q : 32 * q + 4, :].bitcast(I32), tabs_in[32 * q : 32 * q + 4, :])
+        nc.vector.tensor_copy(v_scales[:], tabs_sb[:].indirect(offs_sb[:]))
+        cols = BANK // 16
+        for h in range(HALVES):
+            nc.vector.tensor_copy(v_words[h][:], tab_sb[:].indirect(offs_sb[:, cols * h : cols * (h + 1)]))
+        for hh in range(2):
+            cast_w(nc.scalar.copy, grouped[1, 0], w1_raw[0, hh], hh)
+        quantize(wq[1, 0], grouped[1, 0][:], 0, PASS)
+        nc.vector.tensor_copy(
+            w3s[:].rearrange("p (g t m) -> p g t m", t=PACK, m=PARTS),
+            w3s_raw[:].rearrange("p (g m t) -> p g t m", t=PACK, m=PARTS),
+        )
+        w3q = {0: deal_w3(0)}
+        cast_w(nc.scalar.copy, grouped[2, 0], w2_raw[0, 0], 0)
+        cast_w(nc.vector.tensor_copy, grouped[2, 0], w2_raw[0, 1], 1)
+        quantize(wq[2, 0], grouped[2, 0][:, 0:PASS], 0, PARTS)
+        quantize(wq[2, 0], grouped[2, 0][:, PASS:], PARTS, PASS)
+
+        tanh_sb = [held([PARTS, S], F32, f"tanh{i}") for i in range(TILES)]
+        xq = [mx_tiles(f"xq{b}", P) for b in range(PASSES)]
+        units = TILES * HALVES
+        d3_of = {}
+        low_of = {}
+
+        def products(u):
+            i, h = divmod(u, HALVES)
+            b, t = divmod(i, PACK)
+            c = slice(PARTS * t, PARTS * (t + 1))
+            rhs = v_words[h][:].bitcast(FP8X4)
+            rhs_scale = v_scales[:, BANK * h : BANK * (h + 1)]
+            d1 = psum.tile([PARTS, BANK], F32, name="d1", bufs=2)
+            d2 = psum.tile([PARTS, BANK], F32, name="d2", bufs=3)
+            d3 = psum.tile([PARTS, BANK], F32, name="d3", bufs=3)
+            for acc, (codes, scales) in ((d1, wq[1, b]), (d2, wq[2, b])):
+                nc.tensor.matmul_mx(
+                    out=acc[:], lhsT=codes[:, c].bitcast(FP8X4), lhsT_scale=scales[:, c],
+                    rhs=rhs, rhs_scale=rhs_scale, start=True, stop=True,
+                )
+            nc.tensor.matmul_mx(
+                out=d3[:], lhsT=w3q[b][:, c].bitcast(FP8X4),
+                lhsT_scale=w3s[:, PARTS * i : PARTS * (i + 1)],
+                rhs=rhs, rhs_scale=rhs_scale, start=True, stop=True,
+            )
+            d1_sb = ring.tile([PARTS, BANK], F32, name="d1_sb")
+            nc.scalar.copy(d1_sb[:], d1[:])
+            low = ring.tile([PARTS, BANK], F32, name="low")
+            nc.vector.tensor_tensor(low[:], d2[:], d1_sb[:], ALU.min)
+            d3_of[u] = d3
+            low_of[u] = low
+
+        def features(u):
+            i, h = divmod(u, HALVES)
+            if u == units - 1:
+                z = keep.tile([PARTS, BANK], F32, name="z_last", tag="late", align_bytes=64)
+            else:
+                z = ring.tile([PARTS, BANK], F32, name="z")
+            nc.vector.tensor_tensor(z[:], d3_of[u][:], low_of[u][:], ALU.add)
+            nc.scalar.activation(tanh_sb[i][:, BANK * h : BANK * (h + 1)], z[:], ACT.Tanh)
+
+        def fold_gain(i):
+            b, t = divmod(i, PACK)
+            f = fade_sb[i // 2][:, i % 2, :]
+            nc.gpsimd.tensor_scalar(f, f, gain_sb[:, b, t : t + 1], 0.0, ALU.mult, ALU.add)
+
+        def pick(i, dst, m0, m1):
+            nc.vector.tensor_tensor(
+                dst[:, i % PACK, :], tanh_sb[i][:].indirect(pos_sb[:, m0 // 16 : m1 // 16]),
+                fade_sb[i // 2][:, i % 2, m0:m1], ALU.mult,
+            )
+
+        def weave(dst, src):
+            nc.scalar.copy(
+                dst[:].rearrange("p (c i t) -> p c t i", i=4, t=PACK),
+                src[:].rearrange("p t (c i) -> p c t i", i=4),
+            )
+
+        def deal_wd_words(b, dealt):
+            nc.vector.tensor_copy(
+                dealt[:].bitcast(U16).rearrange("p (a t m) -> p a t m", t=PACK, m=PARTS),
+                wd_raw[:].bitcast(U16).rearrange("p (a b m t) -> p b a t m", a=PASSES, t=PACK, m=PARTS)[:, b],
+            )
+
+        def deal_wd_scales(b, dealt):
+            nc.vector.tensor_copy(
+                dealt[:].rearrange("p (a t m) -> p a t m", t=PACK, m=PARTS),
+                wds_raw[:].rearrange("p (a b m t) -> p b a t m", a=PASSES, t=PACK, m=PARTS)[:, b],
+            )
+
+        sg = held([PARTS, TILES], F32, "sg")
+        x32_0 = held([PARTS, PACK, P], F32, "x32_0")
+        xb_0 = held([PARTS, P * PACK], BF16, "xb_0")
+        x32_a = keep.tile([PARTS, PACK, CHUNK], F32, name="x32_a", tag="x32_a", align_bytes=64)
+        wd_dealt = {0: held([PARTS, PASSES * PASS * 2], U8, "wd_dealt0")}
+        wds_dealt = {0: held([PARTS, PASSES * PASS], U8, "wds_dealt0")}
+
+        products(0)
+        for u in range(units):
+            if u + 1 < units:
+                products(u + 1)
+            features(u)
+            if u % HALVES == 0:
+                fold_gain(u // HALVES)
+            if u % HALVES == 1 and u > 1:
+                i = u // HALVES - 1
+                if i < PACK:
+                    pick(i, x32_0, 0, P)
+                else:
+                    pick(i, x32_a, 0, CHUNK)
+            if u in (1, 2):
+                cast_w(nc.scalar.copy, grouped[1, 1], w1_raw[1, u - 1], u - 1)
+            if u in (3, 4):
+                cast_w(nc.scalar.copy, grouped[2, 1], w2_raw[1, u - 3], u - 3)
+            if u == 3:
+                quantize(wq[1, 1], grouped[1, 1][:], 0, PASS)
+            if u == 5:
+                quantize(wq[2, 1], grouped[2, 1][:], 0, PASS)
+                w3q[1] = deal_w3(1)
+            if u == 10:
+                weave(xb_0, x32_0)
+                deal_wd_words(0, wd_dealt[0])
+                nc.vector.tensor_tensor(
+                    sg[:], skip_sb[:].rearrange("p b t -> p (b t)"), gain_sb[:].rearrange("p b t -> p (b t)"), ALU.mult
+                )
+            if u == 12:
+                quantize(xq[0], xb_0[:], 0, P)
+                deal_wd_scales(0, wds_dealt[0])
+
+        page_of = {}
+
+        def make_page(i):
+            page = pages.tile([PARTS, S], F32, name="page")
+            nc.scalar.activation(page[:], tanh_sb[i][:], ACT.Copy, scale=sg[:, i : i + 1])
+            page_of[i] = page
+
+        def rework(i, m0, m1):
+            b, t = divmod(i, PACK)
+            e = psum.tile([PARTS, BANK], F32, name="d1", bufs=2)
+            for a in range(PASSES):
+                c0 = PASS * a + PARTS * t
+                nc.tensor.matmul_mx(
+                    out=e[:, 0 : m1 - m0], lhsT=wd_dealt[b][:, 2 * c0 : 2 * (c0 + PARTS)].bitcast(FP4X4),
+                    lhsT_scale=wds_dealt[b][:, c0 : c0 + PARTS],
+                    rhs=xq[a][0][:, m0:m1].bitcast(FP8X4), rhs_scale=xq[a][1][:, m0:m1],
+                    start=(a == 0), stop=(a == PASSES - 1),
+                )
+            y = ring.tile([PARTS, P], F32, name="y")
+            nc.scalar.activation(y[:, 0 : m1 - m0], e[:, 0 : m1 - m0], ACT.Sigmoid, bias=base_sb[:, b, t : t + 1])
+            nc.vector.tensor_tensor(
+                page_of[i][:].indirect(pos_sb[:, m0 // 16 : m1 // 16]), y[:, 0 : m1 - m0],
+                wgo_sb[:, t, m0:m1], ALU.mult,
+            )
+
+        def store(i):
+            b, t = divmod(i, PACK)
+            nc.sync.dma_start(
+                out=out[PASS * b : PASS * (b + 1), :].rearrange("(p t) j -> p t j", t=PACK)[:, t, :],
+                in_=page_of[i][:],
+            )
+
+        pick(TILES - 1, x32_a, 0, CHUNK)
+        xb_a = keep.tile([PARTS, CHUNK * PACK], BF16, name="xb_a", tag="xb_a", align_bytes=64)
+        weave(xb_a, x32_a)
+        x32_b = keep.tile([PARTS, PACK, CHUNK], F32, name="x32_b", tag="late", align_bytes=64)
+        for i in range(PACK, TILES):
+            pick(i, x32_b, CHUNK, P)
+        quantize(xq[1], xb_a[:], 0, CHUNK)
+        wd_dealt[1] = keep.tile([PARTS, PASSES * PASS * 2], U8, name="wd_dealt1", tag="xb_a", align_bytes=64)
+        wds_dealt[1] = keep.tile([PARTS, PASSES * PASS], U8, name="wds_dealt1", tag="x32_a", align_bytes=64)
+        deal_wd_scales(1, wds_dealt[1])
+        deal_wd_words(1, wd_dealt[1])
+        for i in range(SPLIT_TILES):
+            make_page(i)
+        rework(0, 0, CHUNK)
+        xb_b = held([PARTS, CHUNK * PACK], BF16, "xb_b")
+        weave(xb_b, x32_b)
+        quantize(xq[1], xb_b[:], CHUNK, P)
+        for i in range(1, SPLIT_TILES):
+            rework(i, 0, CHUNK)
+        for i in range(SPLIT_TILES):
+            rework(i, CHUNK, P)
+            store(i)
+        for i in range(SPLIT_TILES, TILES):
+            make_page(i)
+            rework(i, 0, P)
+            store(i)

@@ -25,6 +25,7 @@ BANK = 512
 HALVES = S // BANK
 CHUNK = P // 2
 SPLIT_TILES = 2
+TWICE_FROM_TILE = 2
 
 
 def tile_list_autochrome_grain_features_kernel(
@@ -51,8 +52,8 @@ def tile_list_autochrome_grain_features_kernel(
         v_words = [held([PARTS, BANK], U32, f"v_words{h}") for h in range(HALVES)]
         v_scales = held([PARTS, S], U8, "v_scales")
 
-        nc.vector.memset(tabs_sb[:].bitcast(I32), 0)
         nc.gpsimd.memset(w3s_raw[:].bitcast(I32), 0)
+        nc.gpsimd.memset(tabs_sb[:].bitcast(I32), 0)
 
         def load_w(w, c0, width, name):
             raw = held([PARTS, PACK, width], F32, name)
@@ -102,9 +103,9 @@ def tile_list_autochrome_grain_features_kernel(
                 out=w3s_raw[32 * q : 32 * q + 4, :].bitcast(I32),
                 in_=w3_scales[0, 4 * q : 4 * q + 4, :].bitcast(I32),
             )
-        w3_raw = {0: load_w3(0)}
         w2_raw[0, 0] = load_w(w2, 0, HW, "w2_raw00")
         w2_raw[0, 1] = load_w(w2, HW, HW, "w2_raw01")
+        w3_raw = {0: load_w3(0)}
         gain_sb = load_vec(gain, "gain_sb")
         nc.sync.dma_start(pos_sb[:], pos1)
         fade_sb = [load_fade(0)]
@@ -170,10 +171,10 @@ def tile_list_autochrome_grain_features_kernel(
             w3s[:].rearrange("p (g t m) -> p g t m", t=PACK, m=PARTS),
             w3s_raw[:].rearrange("p (g m t) -> p g t m", t=PACK, m=PARTS),
         )
-        w3q = {0: deal_w3(0)}
         cast_w(nc.scalar.copy, grouped[2, 0], w2_raw[0, 0], 0)
         cast_w(nc.vector.tensor_copy, grouped[2, 0], w2_raw[0, 1], 1)
         quantize(wq[2, 0], grouped[2, 0][:, 0:PASS], 0, PARTS)
+        w3q = {0: deal_w3(0)}
         quantize(wq[2, 0], grouped[2, 0][:, PASS:], PARTS, PASS)
 
         tanh_sb = [held([PARTS, S], F32, f"tanh{i}") for i in range(TILES)]
@@ -182,39 +183,55 @@ def tile_list_autochrome_grain_features_kernel(
         d3_of = {}
         low_of = {}
 
+        def z_tile(u):
+            if u == units - 1:
+                return keep.tile([PARTS, BANK], F32, name="z_last", tag="late", align_bytes=64)
+            return ring.tile([PARTS, BANK], F32, name="z")
+
+        def d3_twice(u):
+            return u % HALVES == HALVES - 1 and u // HALVES >= TWICE_FROM_TILE
+
         def products(u):
             i, h = divmod(u, HALVES)
             b, t = divmod(i, PACK)
             c = slice(PARTS * t, PARTS * (t + 1))
-            rhs = v_words[h][:].bitcast(FP8X4)
-            rhs_scale = v_scales[:, BANK * h : BANK * (h + 1)]
+
+            def mx_pass(acc, codes, scales, start, stop):
+                nc.tensor.matmul_mx(
+                    out=acc[:], lhsT=codes.bitcast(FP8X4), lhsT_scale=scales,
+                    rhs=v_words[h][:].bitcast(FP8X4), rhs_scale=v_scales[:, BANK * h : BANK * (h + 1)],
+                    start=start, stop=stop,
+                )
+
+            w3_cols = (w3q[b][:, c], w3s[:, PARTS * i : PARTS * (i + 1)])
             d1 = psum.tile([PARTS, BANK], F32, name="d1", bufs=2)
             d2 = psum.tile([PARTS, BANK], F32, name="d2", bufs=3)
-            d3 = psum.tile([PARTS, BANK], F32, name="d3", bufs=3)
             for acc, (codes, scales) in ((d1, wq[1, b]), (d2, wq[2, b])):
-                nc.tensor.matmul_mx(
-                    out=acc[:], lhsT=codes[:, c].bitcast(FP8X4), lhsT_scale=scales[:, c],
-                    rhs=rhs, rhs_scale=rhs_scale, start=True, stop=True,
-                )
-            nc.tensor.matmul_mx(
-                out=d3[:], lhsT=w3q[b][:, c].bitcast(FP8X4),
-                lhsT_scale=w3s[:, PARTS * i : PARTS * (i + 1)],
-                rhs=rhs, rhs_scale=rhs_scale, start=True, stop=True,
-            )
-            d1_sb = ring.tile([PARTS, BANK], F32, name="d1_sb")
+                mx_pass(acc, codes[:, c], scales[:, c], True, not d3_twice(u))
+                if d3_twice(u):
+                    mx_pass(acc, *w3_cols, False, True)
+            if d3_twice(u):
+                low = z_tile(u)
+            else:
+                d3 = psum.tile([PARTS, BANK], F32, name="d3", bufs=3)
+                mx_pass(d3, *w3_cols, True, True)
+                d3_of[u] = d3
+                low = ring.tile([PARTS, BANK], F32, name="low")
+            if u == units - 1:
+                d1_sb = keep.tile([PARTS, BANK], F32, name="d1_last", tag="d1_last", align_bytes=64)
+            else:
+                d1_sb = ring.tile([PARTS, BANK], F32, name="d1_sb")
             nc.scalar.copy(d1_sb[:], d1[:])
-            low = ring.tile([PARTS, BANK], F32, name="low")
             nc.vector.tensor_tensor(low[:], d2[:], d1_sb[:], ALU.min)
-            d3_of[u] = d3
             low_of[u] = low
 
         def features(u):
             i, h = divmod(u, HALVES)
-            if u == units - 1:
-                z = keep.tile([PARTS, BANK], F32, name="z_last", tag="late", align_bytes=64)
+            if d3_twice(u):
+                z = low_of[u]
             else:
-                z = ring.tile([PARTS, BANK], F32, name="z")
-            nc.vector.tensor_tensor(z[:], d3_of[u][:], low_of[u][:], ALU.add)
+                z = z_tile(u)
+                nc.vector.tensor_tensor(z[:], d3_of[u][:], low_of[u][:], ALU.add)
             nc.scalar.activation(tanh_sb[i][:, BANK * h : BANK * (h + 1)], z[:], ACT.Tanh)
 
         def fold_gain(i):
@@ -246,7 +263,7 @@ def tile_list_autochrome_grain_features_kernel(
                 wds_raw[:].rearrange("p (a b m t) -> p b a t m", a=PASSES, t=PACK, m=PARTS)[:, b],
             )
 
-        sg = held([PARTS, TILES], F32, "sg")
+        half_base = held([PARTS, TILES], F32, "half_base")
         x32_0 = held([PARTS, PACK, P], F32, "x32_0")
         xb_0 = held([PARTS, P * PACK], BF16, "xb_0")
         x32_a = keep.tile([PARTS, PACK, CHUNK], F32, name="x32_a", tag="x32_a", align_bytes=64)
@@ -278,13 +295,15 @@ def tile_list_autochrome_grain_features_kernel(
             if u == 10:
                 weave(xb_0, x32_0)
                 deal_wd_words(0, wd_dealt[0])
-                nc.vector.tensor_tensor(
-                    sg[:], skip_sb[:].rearrange("p b t -> p (b t)"), gain_sb[:].rearrange("p b t -> p (b t)"), ALU.mult
-                )
+                nc.scalar.activation(half_base[:], base_sb[:].rearrange("p b t -> p (b t)"), ACT.Copy, scale=0.5)
             if u == 12:
                 quantize(xq[0], xb_0[:], 0, P)
                 deal_wd_scales(0, wds_dealt[0])
 
+        sg = keep.tile([PARTS, TILES], F32, name="sg", tag="d1_last", align_bytes=64)
+        nc.gpsimd.tensor_tensor(
+            sg[:], skip_sb[:].rearrange("p b t -> p (b t)"), gain_sb[:].rearrange("p b t -> p (b t)"), ALU.mult
+        )
         page_of = {}
 
         def make_page(i):
@@ -303,8 +322,12 @@ def tile_list_autochrome_grain_features_kernel(
                     rhs=xq[a][0][:, m0:m1].bitcast(FP8X4), rhs_scale=xq[a][1][:, m0:m1],
                     start=(a == 0), stop=(a == PASSES - 1),
                 )
+            th = ring.tile([PARTS, P], F32, name="th", bufs=2)
+            nc.scalar.activation(
+                th[:, 0 : m1 - m0], e[:, 0 : m1 - m0], ACT.Tanh, bias=half_base[:, i : i + 1], scale=0.5
+            )
             y = ring.tile([PARTS, P], F32, name="y")
-            nc.scalar.activation(y[:, 0 : m1 - m0], e[:, 0 : m1 - m0], ACT.Sigmoid, bias=base_sb[:, b, t : t + 1])
+            nc.scalar.activation(y[:, 0 : m1 - m0], th[:, 0 : m1 - m0], ACT.Copy, bias=0.5, scale=0.5)
             nc.vector.tensor_tensor(
                 page_of[i][:].indirect(pos_sb[:, m0 // 16 : m1 // 16]), y[:, 0 : m1 - m0],
                 wgo_sb[:, t, m0:m1], ALU.mult,

@@ -26,6 +26,7 @@ HALVES = S // BANK
 CHUNK = P // 2
 SPLIT_TILES = 2
 TWICE_FROM_TILE = 2
+HEIRS = {"grp11": 2, "grp21": 4, "w3_dealt1": 5, "wd_dealt0": 9, "wds_dealt0": 10, "x32_b": 15}
 
 
 def tile_list_autochrome_grain_features_kernel(
@@ -42,9 +43,12 @@ def tile_list_autochrome_grain_features_kernel(
         def held(shape, dtype, name):
             return keep.tile(shape, dtype, name=name, align_bytes=64)
 
+        def heir(shape, dtype, name):
+            return keep.tile(shape, dtype, name=name, tag=f"z{HEIRS[name]}", align_bytes=64)
+
         offs_sb = keep.tile([PARTS, S // 16], U16, name="offs_sb")
         pos_sb = keep.tile([PARTS, P // 16], U16, name="pos_sb")
-        tab_sb = held([PARTS, T], U32, "tab_sb")
+        tab_sb = keep.tile([PARTS, T], U32, name="tab_sb", tag="tab", align_bytes=64)
         tabs_sb = held([PARTS, T], U8, "tabs_sb")
         w3s_raw = held([PARTS, H], U8, "w3s_raw")
         w3s = held([PARTS, H], U8, "w3s")
@@ -82,7 +86,7 @@ def tile_list_autochrome_grain_features_kernel(
             )
             return sb
 
-        tabs_in = held([PARTS, T // 4], I32, "tabs_in")
+        tabs_in = keep.tile([PARTS, T // 4], I32, name="tabs_in", tag="tabs_in", align_bytes=64)
         for q in range(4):
             nc.sync.dma_start(
                 out=tabs_in[32 * q : 32 * q + 4, :], in_=tab_scales[0, 4 * q : 4 * q + 4, :].bitcast(I32)
@@ -149,13 +153,13 @@ def tile_list_autochrome_grain_features_kernel(
             nc.vector.quantize_mx(out=tiles[0][:, c0:c1].bitcast(FP8X4), scales=tiles[1][:, c0:c1], in_=src)
 
         def deal_w3(b):
-            dealt = held([PARTS, PASS], I32, f"w3_dealt{b}")
+            dealt = (heir if b else held)([PARTS, PASS], I32, f"w3_dealt{b}")
             nc.vector.tensor_copy(
                 dealt[:].rearrange("p (t m) -> p m t", t=PACK), w3_raw[b][:].rearrange("p (m t) -> p m t", t=PACK)
             )
             return dealt
 
-        grouped = {(n, b): held([PARTS, PACK * PASS], BF16, f"grp{n}{b}") for n in (1, 2) for b in range(PASSES)}
+        grouped = {(n, 0): held([PARTS, PACK * PASS], BF16, f"grp{n}") for n in (1, 2)}
         wq = {(n, b): mx_tiles(f"wq{n}{b}", PASS) for n in (1, 2) for b in range(PASSES)}
 
         for q in range(4):
@@ -164,8 +168,8 @@ def tile_list_autochrome_grain_features_kernel(
         cols = BANK // 16
         for h in range(HALVES):
             nc.vector.tensor_copy(v_words[h][:], tab_sb[:].indirect(offs_sb[:, cols * h : cols * (h + 1)]))
-        for hh in range(2):
-            cast_w(nc.scalar.copy, grouped[1, 0], w1_raw[0, hh], hh)
+        cast_w(nc.scalar.copy, grouped[1, 0], w1_raw[0, 0], 0)
+        cast_w(nc.scalar.copy, grouped[1, 0], w1_raw[0, 1], 1)
         quantize(wq[1, 0], grouped[1, 0][:], 0, PASS)
         nc.vector.tensor_copy(
             w3s[:].rearrange("p (g t m) -> p g t m", t=PACK, m=PARTS),
@@ -184,45 +188,55 @@ def tile_list_autochrome_grain_features_kernel(
         low_of = {}
 
         def z_tile(u):
-            if u == units - 1:
-                return keep.tile([PARTS, BANK], F32, name="z_last", tag="late", align_bytes=64)
+            if u in HEIRS.values():
+                return keep.tile([PARTS, BANK], F32, name=f"z{u}", tag=f"z{u}", align_bytes=64)
             return ring.tile([PARTS, BANK], F32, name="z")
 
         def d3_twice(u):
             return u % HALVES == HALVES - 1 and u // HALVES >= TWICE_FROM_TILE
 
-        def products(u):
+        def mx_pass(u, acc, n, start, stop):
             i, h = divmod(u, HALVES)
             b, t = divmod(i, PACK)
             c = slice(PARTS * t, PARTS * (t + 1))
+            if n == 3:
+                codes, scales = w3q[b][:, c], w3s[:, PARTS * i : PARTS * (i + 1)]
+            else:
+                codes, scales = wq[n, b][0][:, c], wq[n, b][1][:, c]
+            nc.tensor.matmul_mx(
+                out=acc[:], lhsT=codes.bitcast(FP8X4), lhsT_scale=scales,
+                rhs=v_words[h][:].bitcast(FP8X4), rhs_scale=v_scales[:, BANK * h : BANK * (h + 1)],
+                start=start, stop=stop,
+            )
 
-            def mx_pass(acc, codes, scales, start, stop):
-                nc.tensor.matmul_mx(
-                    out=acc[:], lhsT=codes.bitcast(FP8X4), lhsT_scale=scales,
-                    rhs=v_words[h][:].bitcast(FP8X4), rhs_scale=v_scales[:, BANK * h : BANK * (h + 1)],
-                    start=start, stop=stop,
-                )
+        def score(u, n, acc):
+            mx_pass(u, acc, n, True, not d3_twice(u))
+            if d3_twice(u):
+                mx_pass(u, acc, 3, False, True)
 
-            w3_cols = (w3q[b][:, c], w3s[:, PARTS * i : PARTS * (i + 1)])
+        d1_of = {}
+
+        def first_score(u):
             d1 = psum.tile([PARTS, BANK], F32, name="d1", bufs=2)
+            score(u, 1, d1)
+            if u == units - 1:
+                d1_sb = keep.tile([PARTS, BANK], F32, name="d1_last", tag="d1_last", align_bytes=64)
+            else:
+                d1_sb = ring.tile([PARTS, BANK], F32, name="d1_sb", bufs=4)
+            nc.scalar.copy(d1_sb[:], d1[:])
+            d1_of[u] = d1_sb
+
+        def smaller_score(u):
             d2 = psum.tile([PARTS, BANK], F32, name="d2", bufs=3)
-            for acc, (codes, scales) in ((d1, wq[1, b]), (d2, wq[2, b])):
-                mx_pass(acc, codes[:, c], scales[:, c], True, not d3_twice(u))
-                if d3_twice(u):
-                    mx_pass(acc, *w3_cols, False, True)
+            score(u, 2, d2)
             if d3_twice(u):
                 low = z_tile(u)
             else:
                 d3 = psum.tile([PARTS, BANK], F32, name="d3", bufs=3)
-                mx_pass(d3, *w3_cols, True, True)
+                mx_pass(u, d3, 3, True, True)
                 d3_of[u] = d3
                 low = ring.tile([PARTS, BANK], F32, name="low")
-            if u == units - 1:
-                d1_sb = keep.tile([PARTS, BANK], F32, name="d1_last", tag="d1_last", align_bytes=64)
-            else:
-                d1_sb = ring.tile([PARTS, BANK], F32, name="d1_sb")
-            nc.scalar.copy(d1_sb[:], d1[:])
-            nc.vector.tensor_tensor(low[:], d2[:], d1_sb[:], ALU.min)
+            nc.vector.tensor_tensor(low[:], d2[:], d1_of[u][:], ALU.min)
             low_of[u] = low
 
         def features(u):
@@ -234,21 +248,24 @@ def tile_list_autochrome_grain_features_kernel(
                 nc.vector.tensor_tensor(z[:], d3_of[u][:], low_of[u][:], ALU.add)
             nc.scalar.activation(tanh_sb[i][:, BANK * h : BANK * (h + 1)], z[:], ACT.Tanh)
 
+        gf = keep.tile([PARTS, PACK, P], F32, name="gf", tag="tabs_in", align_bytes=64)
+
         def fold_gain(i):
             b, t = divmod(i, PACK)
-            f = fade_sb[i // 2][:, i % 2, :]
-            nc.gpsimd.tensor_scalar(f, f, gain_sb[:, b, t : t + 1], 0.0, ALU.mult, ALU.add)
+            nc.gpsimd.tensor_scalar(
+                gf[:, t, :], fade_sb[i // 2][:, i % 2, :], gain_sb[:, b, t : t + 1], 0.0, ALU.mult, ALU.add
+            )
 
         def pick(i, dst, m0, m1):
             nc.vector.tensor_tensor(
                 dst[:, i % PACK, :], tanh_sb[i][:].indirect(pos_sb[:, m0 // 16 : m1 // 16]),
-                fade_sb[i // 2][:, i % 2, m0:m1], ALU.mult,
+                gf[:, i % PACK, m0:m1], ALU.mult,
             )
 
         def weave(dst, src):
             nc.scalar.copy(
                 dst[:].rearrange("p (c i t) -> p c t i", i=4, t=PACK),
-                src[:].rearrange("p t (c i) -> p c t i", i=4),
+                src.rearrange("p t (c i) -> p c t i", i=4),
             )
 
         def deal_wd_words(b, dealt):
@@ -263,46 +280,55 @@ def tile_list_autochrome_grain_features_kernel(
                 wds_raw[:].rearrange("p (a b m t) -> p b a t m", a=PASSES, t=PACK, m=PARTS)[:, b],
             )
 
-        half_base = held([PARTS, TILES], F32, "half_base")
-        x32_0 = held([PARTS, PACK, P], F32, "x32_0")
-        xb_0 = held([PARTS, P * PACK], BF16, "xb_0")
+        x32_0 = keep.tile([PARTS, PACK, P], F32, name="x32_0", tag="tab", align_bytes=64)
+        xb_0 = [held([PARTS, CHUNK * PACK], BF16, f"xb_0{c}") for c in range(2)]
         x32_a = keep.tile([PARTS, PACK, CHUNK], F32, name="x32_a", tag="x32_a", align_bytes=64)
-        wd_dealt = {0: held([PARTS, PASSES * PASS * 2], U8, "wd_dealt0")}
-        wds_dealt = {0: held([PARTS, PASSES * PASS], U8, "wds_dealt0")}
+        wd_dealt = {}
+        wds_dealt = {}
 
-        products(0)
+        first_score(0)
+        first_score(1)
+        smaller_score(0)
+        for i in range(PACK):
+            fold_gain(i)
         for u in range(units):
+            if u + 2 < units:
+                first_score(u + 2)
             if u + 1 < units:
-                products(u + 1)
+                smaller_score(u + 1)
             features(u)
-            if u % HALVES == 0:
-                fold_gain(u // HALVES)
+            for n, raw in ((1, w1_raw), (2, w2_raw)):
+                if u == HEIRS[f"grp{n}1"]:
+                    grouped[n, 1] = heir([PARTS, PACK * PASS], BF16, f"grp{n}1")
+                    cast_w(nc.scalar.copy, grouped[n, 1], raw[1, 0], 0)
+                    cast_w(nc.vector.tensor_copy, grouped[n, 1], raw[1, 1], 1)
+                if u == HEIRS[f"grp{n}1"] + 1:
+                    quantize(wq[n, 1], grouped[n, 1][:], 0, PASS)
+            if u == HEIRS["w3_dealt1"]:
+                w3q[1] = deal_w3(1)
+            if u == 9:
+                wd_dealt[0] = heir([PARTS, PASSES * PASS * 2], U8, "wd_dealt0")
+                deal_wd_words(0, wd_dealt[0])
+            if u == 10:
+                weave(xb_0[0], x32_0[:, :, 0:CHUNK])
+                wds_dealt[0] = heir([PARTS, PASSES * PASS], U8, "wds_dealt0")
+                deal_wd_scales(0, wds_dealt[0])
+            if u == 12:
+                quantize(xq[0], xb_0[0][:], 0, CHUNK)
             if u % HALVES == 1 and u > 1:
                 i = u // HALVES - 1
                 if i < PACK:
                     pick(i, x32_0, 0, P)
+                    fold_gain(i + PACK)
                 else:
                     pick(i, x32_a, 0, CHUNK)
-            if u in (1, 2):
-                cast_w(nc.scalar.copy, grouped[1, 1], w1_raw[1, u - 1], u - 1)
-            if u in (3, 4):
-                cast_w(nc.scalar.copy, grouped[2, 1], w2_raw[1, u - 3], u - 3)
-            if u == 3:
-                quantize(wq[1, 1], grouped[1, 1][:], 0, PASS)
-            if u == 5:
-                quantize(wq[2, 1], grouped[2, 1][:], 0, PASS)
-                w3q[1] = deal_w3(1)
-            if u == 10:
-                weave(xb_0, x32_0)
-                deal_wd_words(0, wd_dealt[0])
-                nc.scalar.activation(half_base[:], base_sb[:].rearrange("p b t -> p (b t)"), ACT.Copy, scale=0.5)
-            if u == 12:
-                quantize(xq[0], xb_0[:], 0, P)
-                deal_wd_scales(0, wds_dealt[0])
 
-        sg = keep.tile([PARTS, TILES], F32, name="sg", tag="d1_last", align_bytes=64)
-        nc.gpsimd.tensor_tensor(
-            sg[:], skip_sb[:].rearrange("p b t -> p (b t)"), gain_sb[:].rearrange("p b t -> p (b t)"), ALU.mult
+        rows = keep.tile([PARTS, 2, TILES], F32, name="rows", tag="d1_last", align_bytes=64)
+        sg = rows[:, 0, :]
+        half_base = rows[:, 1, :]
+        nc.scalar.activation(half_base, base_sb[:].rearrange("p b t -> p (b t)"), ACT.Copy, scale=0.5)
+        nc.vector.tensor_tensor(
+            sg, skip_sb[:].rearrange("p b t -> p (b t)"), gain_sb[:].rearrange("p b t -> p (b t)"), ALU.mult
         )
         page_of = {}
 
@@ -342,8 +368,8 @@ def tile_list_autochrome_grain_features_kernel(
 
         pick(TILES - 1, x32_a, 0, CHUNK)
         xb_a = keep.tile([PARTS, CHUNK * PACK], BF16, name="xb_a", tag="xb_a", align_bytes=64)
-        weave(xb_a, x32_a)
-        x32_b = keep.tile([PARTS, PACK, CHUNK], F32, name="x32_b", tag="late", align_bytes=64)
+        weave(xb_a, x32_a[:])
+        x32_b = heir([PARTS, PACK, CHUNK], F32, "x32_b")
         for i in range(PACK, TILES):
             pick(i, x32_b, CHUNK, P)
         quantize(xq[1], xb_a[:], 0, CHUNK)
@@ -355,7 +381,9 @@ def tile_list_autochrome_grain_features_kernel(
             make_page(i)
         rework(0, 0, CHUNK)
         xb_b = held([PARTS, CHUNK * PACK], BF16, "xb_b")
-        weave(xb_b, x32_b)
+        weave(xb_0[1], x32_0[:, :, CHUNK:P])
+        weave(xb_b, x32_b[:])
+        quantize(xq[0], xb_0[1][:], CHUNK, P)
         quantize(xq[1], xb_b[:], CHUNK, P)
         for i in range(1, SPLIT_TILES):
             rework(i, 0, CHUNK)

from contextlib import ExitStack

import concourse.mybir as mybir

K, T, S, H, P = 512, 4096, 1024, 1024, 512
FLOPS = 2 * (3 * K * H * S + H * H * P)

F32 = mybir.dt.float32
BF16 = mybir.dt.bfloat16
I32 = mybir.dt.int32
U32 = mybir.dt.uint32
U16 = mybir.dt.uint16
U8 = mybir.dt.uint8
FP8X4 = mybir.dt.float8_e4m3fn_x4
FP4X4 = mybir.dt.float4_e2m1fn_x4
ALU = mybir.AluOpType
ACT = mybir.ActivationFunctionType

PARTS = 128
PACK = 4
PASS = PARTS * PACK
PASSES = H // PASS
TILES = H // PARTS
BANK = 512
HALVES = S // BANK
CHUNK = P // 2
SPLIT_TILES = 2
TWICE_FROM_TILE = 2
HEIRS = {"grp11": 2, "grp21": 4, "w3_dealt1": 5, "wd_dealt0": 9, "wds_dealt0": 10, "x32_b": 15}


def tile_list_autochrome_grain_features_kernel(
    tc, tab_words, tab_scales, offs, pos1, w1, w2, w3_words, w3_scales,
    gain, fade, wd_words, wd_scales, base, skip, wgo, out,
):
    nc = tc.nc
    with ExitStack() as ctx:
        keep = ctx.enter_context(tc.tile_pool(name="keep", bufs=1))
        ring = ctx.enter_context(tc.tile_pool(name="ring", bufs=3))
        pages = ctx.enter_context(tc.tile_pool(name="pages", bufs=4))
        psum = ctx.enter_context(tc.psum_pool(name="psum", bufs=1))

        def held(shape, dtype, name):
            return keep.tile(shape, dtype, name=name, align_bytes=64)

        def heir(shape, dtype, name):
            return keep.tile(shape, dtype, name=name, tag=f"z{HEIRS[name]}", align_bytes=64)

        offs_sb = keep.tile([PARTS, S // 16], U16, name="offs_sb")
        pos_sb = keep.tile([PARTS, P // 16], U16, name="pos_sb")
        tab_sb = keep.tile([PARTS, T], U32, name="tab_sb", tag="tab", align_bytes=64)
        tabs_sb = held([PARTS, T], U8, "tabs_sb")
        w3s_raw = held([PARTS, H], U8, "w3s_raw")
        w3s = held([PARTS, H], U8, "w3s")
        wds_raw = held([PARTS, PASSES * H], U8, "wds_raw")
        v_words = [held([PARTS, BANK], U32, f"v_words{h}") for h in range(HALVES)]
        v_scales = held([PARTS, S], U8, "v_scales")

        nc.gpsimd.memset(w3s_raw[:].bitcast(I32), 0)
        nc.gpsimd.memset(tabs_sb[:].bitcast(I32), 0)

        def load_w(w, c0, width, name):
            raw = held([PARTS, PACK, width], F32, name)
            nc.sync.dma_start(out=raw[:], in_=w[:, c0 : c0 + width].rearrange("(p j) c -> p j c", j=PACK))
            return raw

        def load_w3(b):
            raw = held([PARTS, PASS], I32, f"w3_raw{b}")
            nc.sync.dma_start(
                out=raw[:],
                in_=w3_words[0].rearrange("p c i -> p (c i)")[:, 4 * PASS * b : 4 * PASS * (b + 1)].bitcast(I32),
            )
            return raw

        def load_vec(vec, name):
            sb = held([PARTS, PASSES, PACK], F32, name)
            nc.sync.dma_start(out=sb[:], in_=vec.rearrange("(b p t) -> p b t", b=PASSES, t=PACK))
            return sb

        def load_fade(pair):
            b, t = divmod(2 * pair, PACK)
            sb = held([PARTS, 2, P], F32, f"fade{pair}")
            nc.sync.dma_start(
                out=sb[:],
                in_=fade[PASS * b : PASS * (b + 1), :].rearrange("(p t) m -> p t m", t=PACK)[:, t : t + 2, :],
            )
            return sb

        tabs_in = keep.tile([PARTS, T // 4], I32, name="tabs_in", tag="tabs_in", align_bytes=64)
        for q in range(4):
            nc.sync.dma_start(
                out=tabs_in[32 * q : 32 * q + 4, :], in_=tab_scales[0, 4 * q : 4 * q + 4, :].bitcast(I32)
            )
        nc.gpsimd.memset(wds_raw[:].bitcast(I32), 0)

        HW = PASS // 2
        w1_raw = {}
        w2_raw = {}
        nc.sync.dma_start(offs_sb[:], offs)
        nc.sync.dma_start(
            out=tab_sb[:].bitcast(I32), in_=tab_words[0].rearrange("p t i -> p (t i)").bitcast(I32)
        )
        w1_raw[0, 0] = load_w(w1, 0, HW, "w1_raw00")
        w1_raw[0, 1] = load_w(w1, HW, HW, "w1_raw01")
        for q in range(4):
            nc.sync.dma_start(
                out=w3s_raw[32 * q : 32 * q + 4, :].bitcast(I32),
                in_=w3_scales[0, 4 * q : 4 * q + 4, :].bitcast(I32),
            )
        w2_raw[0, 0] = load_w(w2, 0, HW, "w2_raw00")
        w2_raw[0, 1] = load_w(w2, HW, HW, "w2_raw01")
        w3_raw = {0: load_w3(0)}
        gain_sb = load_vec(gain, "gain_sb")
        nc.sync.dma_start(pos_sb[:], pos1)
        fade_sb = [load_fade(0)]
        for hh in range(2):
            w1_raw[1, hh] = load_w(w1, PASS + hh * HW, HW, f"w1_raw1{hh}")
        fade_sb.append(load_fade(1))
        for hh in range(2):
            w2_raw[1, hh] = load_w(w2, PASS + hh * HW, HW, f"w2_raw1{hh}")
        w3_raw[1] = load_w3(1)
        fade_sb.append(load_fade(2))
        fade_sb.append(load_fade(3))
        skip_sb = load_vec(skip, "skip_sb")
        base_sb = load_vec(base, "base_sb")
        wd_raw = held([PARTS, PASSES * H * 2], U8, "wd_raw")
        nc.sync.dma_start(
            out=wd_raw[:].bitcast(I32).rearrange("p (a n) -> p a n", a=PASSES),
            in_=wd_words.bitcast(I32).rearrange("a p n -> p a n"),
        )
        for q in range(4):
            nc.sync.dma_start(
                out=wds_raw[32 * q : 32 * q + 4, :].bitcast(I32).rearrange("r (a n) -> r a n", a=PASSES),
                in_=wd_scales[:, 4 * q : 4 * q + 4, :].bitcast(I32).rearrange("a r n -> r a n"),
            )
        wgo_sb = held([PARTS, PACK, P], F32, "wgo_sb")
        for q in range(4):
            nc.sync.dma_start(
                out=wgo_sb[32 * q : 32 * q + 32], in_=wgo.rearrange("(p t) m -> p t m", t=PACK)
            )

        def cast_w(engine_copy, grouped, raw, hh):
            mm = PARTS // 2
            engine_copy(
                grouped[:].rearrange("p (t m j) -> p m j t", t=PACK, j=PACK)[:, mm * hh : mm * (hh + 1)],
                raw[:].rearrange("p j (m t) -> p m j t", t=PACK),
            )

        def mx_tiles(name, width):
            return held([PARTS, width], U32, name + "_codes"), held([PARTS, width], U8, name + "_scales")

        def quantize(tiles, src, c0, c1):
            nc.vector.quantize_mx(out=tiles[0][:, c0:c1].bitcast(FP8X4), scales=tiles[1][:, c0:c1], in_=src)

        def deal_w3(b):
            dealt = (heir if b else held)([PARTS, PASS], I32, f"w3_dealt{b}")
            nc.vector.tensor_copy(
                dealt[:].rearrange("p (t m) -> p m t", t=PACK), w3_raw[b][:].rearrange("p (m t) -> p m t", t=PACK)
            )
            return dealt

        grouped = {(n, 0): held([PARTS, PACK * PASS], BF16, f"grp{n}") for n in (1, 2)}
        wq = {(n, b): mx_tiles(f"wq{n}{b}", PASS) for n in (1, 2) for b in range(PASSES)}

        for q in range(4):
            nc.vector.tensor_copy(tabs_sb[32 * q : 32 * q + 4, :].bitcast(I32), tabs_in[32 * q : 32 * q + 4, :])
        nc.vector.tensor_copy(v_scales[:], tabs_sb[:].indirect(offs_sb[:]))
        cols = BANK // 16
        for h in range(HALVES):
            nc.vector.tensor_copy(v_words[h][:], tab_sb[:].indirect(offs_sb[:, cols * h : cols * (h + 1)]))
        cast_w(nc.scalar.copy, grouped[1, 0], w1_raw[0, 0], 0)
        cast_w(nc.scalar.copy, grouped[1, 0], w1_raw[0, 1], 1)
        quantize(wq[1, 0], grouped[1, 0][:], 0, PASS)
        nc.vector.tensor_copy(
            w3s[:].rearrange("p (g t m) -> p g t m", t=PACK, m=PARTS),
            w3s_raw[:].rearrange("p (g m t) -> p g t m", t=PACK, m=PARTS),
        )
        cast_w(nc.scalar.copy, grouped[2, 0], w2_raw[0, 0], 0)
        cast_w(nc.vector.tensor_copy, grouped[2, 0], w2_raw[0, 1], 1)
        quantize(wq[2, 0], grouped[2, 0][:, 0:PASS], 0, PARTS)
        w3q = {0: deal_w3(0)}
        quantize(wq[2, 0], grouped[2, 0][:, PASS:], PARTS, PASS)

        tanh_sb = [held([PARTS, S], F32, f"tanh{i}") for i in range(TILES)]
        xq = [mx_tiles(f"xq{b}", P) for b in range(PASSES)]
        units = TILES * HALVES
        d3_of = {}
        low_of = {}

        def z_tile(u):
            if u in HEIRS.values():
                return keep.tile([PARTS, BANK], F32, name=f"z{u}", tag=f"z{u}", align_bytes=64)
            return ring.tile([PARTS, BANK], F32, name="z")

        def d3_twice(u):
            return u % HALVES == HALVES - 1 and u // HALVES >= TWICE_FROM_TILE

        def mx_pass(u, acc, n, start, stop):
            i, h = divmod(u, HALVES)
            b, t = divmod(i, PACK)
            c = slice(PARTS * t, PARTS * (t + 1))
            if n == 3:
                codes, scales = w3q[b][:, c], w3s[:, PARTS * i : PARTS * (i + 1)]
            else:
                codes, scales = wq[n, b][0][:, c], wq[n, b][1][:, c]
            nc.tensor.matmul_mx(
                out=acc[:], lhsT=codes.bitcast(FP8X4), lhsT_scale=scales,
                rhs=v_words[h][:].bitcast(FP8X4), rhs_scale=v_scales[:, BANK * h : BANK * (h + 1)],
                start=start, stop=stop,
            )

        def score(u, n, acc):
            mx_pass(u, acc, n, True, not d3_twice(u))
            if d3_twice(u):
                mx_pass(u, acc, 3, False, True)

        d1_of = {}

        def first_score(u):
            d1 = psum.tile([PARTS, BANK], F32, name="d1", bufs=2)
            score(u, 1, d1)
            if u == units - 1:
                d1_sb = keep.tile([PARTS, BANK], F32, name="d1_last", tag="d1_last", align_bytes=64)
            else:
                d1_sb = ring.tile([PARTS, BANK], F32, name="d1_sb", bufs=4)
            nc.scalar.copy(d1_sb[:], d1[:])
            d1_of[u] = d1_sb

        def smaller_score(u):
            d2 = psum.tile([PARTS, BANK], F32, name="d2", bufs=3)
            score(u, 2, d2)
            if d3_twice(u):
                low = z_tile(u)
            else:
                d3 = psum.tile([PARTS, BANK], F32, name="d3", bufs=3)
                mx_pass(u, d3, 3, True, True)
                d3_of[u] = d3
                low = ring.tile([PARTS, BANK], F32, name="low")
            nc.vector.tensor_tensor(low[:], d2[:], d1_of[u][:], ALU.min)
            low_of[u] = low

        def features(u):
            i, h = divmod(u, HALVES)
            if d3_twice(u):
                z = low_of[u]
            else:
                z = z_tile(u)
                nc.vector.tensor_tensor(z[:], d3_of[u][:], low_of[u][:], ALU.add)
            nc.scalar.activation(tanh_sb[i][:, BANK * h : BANK * (h + 1)], z[:], ACT.Tanh)

        gf = keep.tile([PARTS, PACK, P], F32, name="gf", tag="tabs_in", align_bytes=64)

        def fold_gain(i):
            b, t = divmod(i, PACK)
            nc.gpsimd.tensor_scalar(
                gf[:, t, :], fade_sb[i // 2][:, i % 2, :], gain_sb[:, b, t : t + 1], 0.0, ALU.mult, ALU.add
            )

        def pick(i, dst, m0, m1):
            nc.vector.tensor_tensor(
                dst[:, i % PACK, :], tanh_sb[i][:].indirect(pos_sb[:, m0 // 16 : m1 // 16]),
                gf[:, i % PACK, m0:m1], ALU.mult,
            )

        def weave(dst, src):
            nc.scalar.copy(
                dst[:].rearrange("p (c i t) -> p c t i", i=4, t=PACK),
                src.rearrange("p t (c i) -> p c t i", i=4),
            )

        def deal_wd_words(b, dealt):
            nc.vector.tensor_copy(
                dealt[:].bitcast(U16).rearrange("p (a t m) -> p a t m", t=PACK, m=PARTS),
                wd_raw[:].bitcast(U16).rearrange("p (a b m t) -> p b a t m", a=PASSES, t=PACK, m=PARTS)[:, b],
            )

        def deal_wd_scales(b, dealt):
            nc.vector.tensor_copy(
                dealt[:].rearrange("p (a t m) -> p a t m", t=PACK, m=PARTS),
                wds_raw[:].rearrange("p (a b m t) -> p b a t m", a=PASSES, t=PACK, m=PARTS)[:, b],
            )

        x32_0 = keep.tile([PARTS, PACK, P], F32, name="x32_0", tag="tab", align_bytes=64)
        xb_0 = [held([PARTS, CHUNK * PACK], BF16, f"xb_0{c}") for c in range(2)]
        x32_a = keep.tile([PARTS, PACK, CHUNK], F32, name="x32_a", tag="x32_a", align_bytes=64)
        wd_dealt = {}
        wds_dealt = {}

        first_score(0)
        first_score(1)
        smaller_score(0)
        for i in range(PACK):
            fold_gain(i)
        for u in range(units):
            if u + 2 < units:
                first_score(u + 2)
            if u + 1 < units:
                smaller_score(u + 1)
            features(u)
            for n, raw in ((1, w1_raw), (2, w2_raw)):
                if u == HEIRS[f"grp{n}1"]:
                    grouped[n, 1] = heir([PARTS, PACK * PASS], BF16, f"grp{n}1")
                    cast_w(nc.scalar.copy, grouped[n, 1], raw[1, 0], 0)
                    cast_w(nc.vector.tensor_copy, grouped[n, 1], raw[1, 1], 1)
                if u == HEIRS[f"grp{n}1"] + 1:
                    quantize(wq[n, 1], grouped[n, 1][:], 0, PASS)
            if u == HEIRS["w3_dealt1"]:
                w3q[1] = deal_w3(1)
            if u == 9:
                wd_dealt[0] = heir([PARTS, PASSES * PASS * 2], U8, "wd_dealt0")
                deal_wd_words(0, wd_dealt[0])
            if u == 10:
                weave(xb_0[0], x32_0[:, :, 0:CHUNK])
                wds_dealt[0] = heir([PARTS, PASSES * PASS], U8, "wds_dealt0")
                deal_wd_scales(0, wds_dealt[0])
            if u == 12:
                quantize(xq[0], xb_0[0][:], 0, CHUNK)
            if u % HALVES == 1 and u > 1:
                i = u // HALVES - 1
                if i < PACK:
                    pick(i, x32_0, 0, P)
                    fold_gain(i + PACK)
                else:
                    pick(i, x32_a, 0, CHUNK)

        rows = keep.tile([PARTS, 2, TILES], F32, name="rows", tag="d1_last", align_bytes=64)
        sg = rows[:, 0, :]
        half_base = rows[:, 1, :]
        nc.scalar.activation(half_base, base_sb[:].rearrange("p b t -> p (b t)"), ACT.Copy, scale=0.5)
        nc.vector.tensor_tensor(
            sg, skip_sb[:].rearrange("p b t -> p (b t)"), gain_sb[:].rearrange("p b t -> p (b t)"), ALU.mult
        )
        page_of = {}

        def make_page(i):
            page = pages.tile([PARTS, S], F32, name="page")
            nc.scalar.activation(page[:], tanh_sb[i][:], ACT.Copy, scale=sg[:, i : i + 1])
            page_of[i] = page

        def rework(i, m0, m1):
            b, t = divmod(i, PACK)
            e = psum.tile([PARTS, BANK], F32, name="d1", bufs=2)
            for a in range(PASSES):
                c0 = PASS * a + PARTS * t
                nc.tensor.matmul_mx(
                    out=e[:, 0 : m1 - m0], lhsT=wd_dealt[b][:, 2 * c0 : 2 * (c0 + PARTS)].bitcast(FP4X4),
                    lhsT_scale=wds_dealt[b][:, c0 : c0 + PARTS],
                    rhs=xq[a][0][:, m0:m1].bitcast(FP8X4), rhs_scale=xq[a][1][:, m0:m1],
                    start=(a == 0), stop=(a == PASSES - 1),
                )
            th = ring.tile([PARTS, P], F32, name="th", bufs=2)
            nc.scalar.activation(
                th[:, 0 : m1 - m0], e[:, 0 : m1 - m0], ACT.Tanh, bias=half_base[:, i : i + 1], scale=0.5
            )
            y = ring.tile([PARTS, P], F32, name="y")
            nc.scalar.activation(y[:, 0 : m1 - m0], th[:, 0 : m1 - m0], ACT.Copy, bias=0.5, scale=0.5)
            nc.vector.tensor_tensor(
                page_of[i][:].indirect(pos_sb[:, m0 // 16 : m1 // 16]), y[:, 0 : m1 - m0],
                wgo_sb[:, t, m0:m1], ALU.mult,
            )

        def store(i):
            b, t = divmod(i, PACK)
            nc.sync.dma_start(
                out=out[PASS * b : PASS * (b + 1), :].rearrange("(p t) j -> p t j", t=PACK)[:, t, :],
                in_=page_of[i][:],
            )

        pick(TILES - 1, x32_a, 0, CHUNK)
        xb_a = keep.tile([PARTS, CHUNK * PACK], BF16, name="xb_a", tag="xb_a", align_bytes=64)
        weave(xb_a, x32_a[:])
        x32_b = heir([PARTS, PACK, CHUNK], F32, "x32_b")
        for i in range(PACK, TILES):
            pick(i, x32_b, CHUNK, P)
        quantize(xq[1], xb_a[:], 0, CHUNK)
        wd_dealt[1] = keep.tile([PARTS, PASSES * PASS * 2], U8, name="wd_dealt1", tag="xb_a", align_bytes=64)
        wds_dealt[1] = keep.tile([PARTS, PASSES * PASS], U8, name="wds_dealt1", tag="x32_a", align_bytes=64)
        deal_wd_scales(1, wds_dealt[1])
        deal_wd_words(1, wd_dealt[1])
        for i in range(SPLIT_TILES):
            make_page(i)
        rework(0, 0, CHUNK)
        xb_b = held([PARTS, CHUNK * PACK], BF16, "xb_b")
        weave(xb_0[1], x32_0[:, :, CHUNK:P])
        weave(xb_b, x32_b[:])
        quantize(xq[0], xb_0[1][:], CHUNK, P)
        quantize(xq[1], xb_b[:], CHUNK, P)
        for i in range(1, SPLIT_TILES):
            rework(i, 0, CHUNK)
        for i in range(SPLIT_TILES):
            rework(i, CHUNK, P)
            store(i)
        for i in range(SPLIT_TILES, TILES):
            make_page(i)
            rework(i, 0, P)
            store(i)
